import numpy as np
import ml_dtypes


def mxq(x, axis, fmt="e4m3"):
    dtype, down = {"e4m3": (ml_dtypes.float8_e4m3fn, 7), "e5m2": (ml_dtypes.float8_e5m2, 14)}[fmt]
    v = np.moveaxis(np.asarray(x, np.float32).astype(ml_dtypes.bfloat16).astype(np.float64), axis, -1)
    blocks = v.reshape(v.shape[:-1] + (-1, 32))
    amax = np.abs(blocks).max(-1, keepdims=True)
    byte = np.maximum(np.where(amax > 0, np.frexp(amax)[1] - 1 + 127, 0) - down, 1)
    scale = np.exp2(byte - 127.0)
    codes = (blocks / scale).astype(np.float32).astype(dtype).astype(np.float64)
    return np.moveaxis((codes * scale).reshape(v.shape), -1, axis)


WIDE = False


def mx_kscale(k):
    if not WIDE:
        return np.ones(k)
    levels = np.array([10, -10, 5, -5, 0])
    if k % 512:
        return np.exp2(np.random.permutation(np.resize(levels, k // 32))).repeat(32)
    a = np.empty((k // 512, 16))
    for p in range(k // 512):
        a[p, :8] = np.random.permutation(np.resize(levels, 8))
        for g in range(8):
            far = levels[np.abs(levels - a[p, g]) >= 10]
            a[p, g + 8] = far[np.random.randint(len(far))]
    return np.exp2(a.ravel()).repeat(32)


def f64(x):
    return np.asarray(x).astype(np.float64)


def striped(idx):
    return np.tile(idx.reshape(-1, 16).T, (8, 1)).astype(np.uint16)


def unstriped(offs):
    return offs[:16].T.reshape(-1).astype(np.int64)


def pack_weight(w):
    k, n = w.shape
    w = f64(np.asarray(w, np.float32).astype(ml_dtypes.bfloat16)).reshape(k // 32, 32, n)
    amax = np.abs(w).max(1)
    byte = np.clip(np.where(amax > 0, np.frexp(amax)[1] - 1 + 127 - 7, 1), 1, 254)
    scaled = (w * np.exp2(127.0 - byte)[:, None, :]).reshape(k, n).astype(np.float32)
    words = np.ascontiguousarray(scaled.reshape(k // 512, 128, 4, n).transpose(0, 1, 3, 2)).astype(ml_dtypes.float8_e4m3fn).view(np.uint8)
    return words, np.ascontiguousarray(byte.astype(np.uint8).reshape(k // 512, 16, n))


def unpack_weight(words, scales):
    g, p, n, _ = words.shape
    vals = np.ascontiguousarray(words).view(ml_dtypes.float8_e4m3fn).astype(np.float64) * np.repeat(np.exp2(scales.astype(np.float64) - 127.0), 8, axis=1)[..., None]
    return vals.transpose(0, 1, 3, 2).reshape(g * 512, n)


def gelu(v):
    return 0.5 * v * (1.0 + np.tanh(np.sqrt(2.0 / np.pi) * (v + 0.044715 * v**3)))


K, T, S, N = 1536, 2048, 512, 128


def setup_inputs():
    n = np.random.standard_normal
    s = mx_kscale(K)[:, None]
    words, scales = pack_weight(n((K, N)) / np.sqrt(K) / s)
    return {
        "xT": (n((K, T)) * s).astype(np.float32),
        "w_words": words,
        "w_scales": scales,
        "b": (0.3 * n((N, 1))).astype(np.float32),
        "offs": striped(np.random.permutation(T)[:S]),
    }


def reference(xT, w_words, w_scales, b, offs):
    w = unpack_weight(w_words, w_scales)
    idx = unstriped(offs)
    xq = mxq(f64(xT)[:, idx], 0, "e4m3")
    y = w.T @ xq
    y = gelu(y + f64(b))
    return y

@@ -1,0 +1,109 @@
+from contextlib import ExitStack
+
+import concourse.mybir as mybir
+
+K, T, S, N = 1536, 2048, 512, 128
+FLOPS = 2 * K * S * N
+
+F32 = mybir.dt.float32
+BF16 = mybir.dt.bfloat16
+I32 = mybir.dt.int32
+U32 = mybir.dt.uint32
+U16 = mybir.dt.uint16
+U8 = mybir.dt.uint8
+FP8X4 = mybir.dt.float8_e4m3fn_x4
+
+P = 128
+PACK = 4
+K_PASS = P * PACK
+PASSES = K // K_PASS
+HALF = S // 2
+LOAD_WIDTHS = ((2, 2), (2, 1, 1), (1, 1, 1, 1))
+
+
+def tile_picked_pick_lin_gelu_sub_e_kernel(tc, xT, w_words, w_scales, b, offs, out):
+    nc = tc.nc
+    gelu = mybir.ActivationFunctionType.Gelu_apprx_tanh
+
+    with ExitStack() as ctx:
+        keep = ctx.enter_context(tc.tile_pool(name="keep", bufs=1))
+        psum = ctx.enter_context(tc.psum_pool(name="psum", bufs=1))
+
+        offsets = keep.tile([P, S // 16], U16, name="offsets")
+        bias = keep.tile([P, 1], F32, name="bias")
+        w_codes = keep.tile([P, PASSES, N], U32, name="w_codes", align_bytes=64)
+        w_planes = keep.tile([P, PASSES, N], U8, name="w_planes", align_bytes=64)
+        warm = keep.tile([P, 1], F32, name="warm")
+        warm_out = keep.tile([P, 1], F32, name="warm_out")
+
+        planes_of = []
+        first_load = True
+        for a in range(PASSES):
+            views = []
+            r = 0
+            for width in LOAD_WIDTHS[a]:
+                raw = keep.tile([P, width, T], F32, name=f"raw_{a}_{r}")
+                src = xT[a * K_PASS : (a + 1) * K_PASS, :].rearrange("(p r) t -> p r t", r=PACK)
+                nc.sync.dma_start(out=raw[:], in_=src[:, r : r + width, :])
+                if first_load:
+                    nc.sync.dma_start(offsets[:], offs)
+                    nc.sync.dma_start(out=bias[:], in_=b)
+                    first_load = False
+                views.extend(raw[:, i, :] for i in range(width))
+                r += width
+            planes_of.append(views)
+        nc.gpsimd.memset(w_planes[:], 0)
+        scales_i32 = w_scales.bitcast(I32).rearrange("a q m -> q a m")
+        for q in range(4):
+            nc.sync.dma_start(out=w_planes[32 * q : 32 * q + 4, :, :].bitcast(I32), in_=scales_i32[4 * q : 4 * q + 4])
+        for a in range(PASSES):
+            nc.sync.dma_start(out=w_codes[:, a, :].bitcast(I32), in_=w_words[a].rearrange("p m r -> p (m r)").bitcast(I32))
+
+        nc.vector.memset(warm[:], 0.0)
+        nc.scalar.activation(warm_out[:], warm[:], gelu)
+
+        grouped = [keep.tile([P, S, PACK], BF16, name=f"grouped_{a}", align_bytes=64) for a in range(PASSES)]
+        codes = [keep.tile([P, S], U32, name=f"codes_{a}", align_bytes=64) for a in range(PASSES)]
+        planes = [keep.tile([P, S], U8, name=f"planes_{a}", align_bytes=64) for a in range(PASSES)]
+        sums = [psum.tile([N, HALF], F32, name=f"sums_{h}") for h in range(2)]
+
+        def pick(a, r, c0, c1):
+            nc.vector.tensor_copy(grouped[a][:, c0:c1, r], planes_of[a][r].indirect(offsets[:, c0 // 16 : c1 // 16]))
+
+        def quantise(a, c0, c1):
+            nc.vector.quantize_mx(
+                out=codes[a][:, c0:c1].bitcast(FP8X4),
+                scales=planes[a][:, c0:c1],
+                in_=grouped[a][:, c0:c1, :].rearrange("p c r -> p (c r)"),
+            )
+
+        def multiply(a, h):
+            cols = slice(h * HALF, (h + 1) * HALF)
+            nc.tensor.matmul_mx(
+                out=sums[h][:],
+                lhsT=w_codes[:, a, :].bitcast(FP8X4),
+                lhsT_scale=w_planes[:, a, :],
+                rhs=codes[a][:, cols].bitcast(FP8X4),
+                rhs_scale=planes[a][:, cols],
+                start=(a == 0),
+                stop=(a == PASSES - 1),
+            )
+
+        for a in range(PASSES - 1):
+            for r in range(PACK):
+                pick(a, r, 0, S)
+            quantise(a, 0, S)
+            for h in range(2):
+                multiply(a, h)
+
+        a = PASSES - 1
+        for r in range(PACK - 1):
+            pick(a, r, 0, S)
+        for h in range(2):
+            pick(a, PACK - 1, h * HALF, (h + 1) * HALF)
+        for h in range(2):
+            quantise(a, h * HALF, (h + 1) * HALF)
+            multiply(a, h)
+            result = keep.tile([N, HALF], F32, name=f"result_{h}")
+            nc.scalar.activation(result[:], sums[h][:], gelu, bias=bias[:])
+            nc.sync.dma_start(out=out[:, h * HALF : (h + 1) * HALF], in_=result[:])

@@ -18,7 +18,12 @@ PACK = 4
 K_PASS = P * PACK
 PASSES = K // K_PASS
 HALF = S // 2
-LOAD_WIDTHS = ((2, 2), (2, 1, 1), (1, 1, 1, 1))
+GROUPS = 4
+GROUP = S // GROUPS
+BLOCK = 32
+LOAD_WIDTHS = ((4,), (2, 2), (2, 1, 1))
+WOVEN_ON_SCALAR = (2, 2, 2)
+RUN = 4
 
 
 def tile_picked_pick_lin_gelu_sub_e_kernel(tc, xT, w_words, w_scales, b, offs, out):
@@ -30,11 +35,15 @@ def tile_picked_pick_lin_gelu_sub_e_kernel(tc, xT, w_words, w_scales, b, offs, o
         psum = ctx.enter_context(tc.psum_pool(name="psum", bufs=1))
 
         offsets = keep.tile([P, S // 16], U16, name="offsets")
-        bias = keep.tile([P, 1], F32, name="bias")
+        bias_rows = keep.tile([P, BLOCK], F32, name="bias_rows", align_bytes=64)
+        bias = keep.tile([P, BLOCK], F32, name="bias", align_bytes=64)
         w_codes = keep.tile([P, PASSES, N], U32, name="w_codes", align_bytes=64)
         w_planes = keep.tile([P, PASSES, N], U8, name="w_planes", align_bytes=64)
-        warm = keep.tile([P, 1], F32, name="warm")
-        warm_out = keep.tile([P, 1], F32, name="warm_out")
+
+        nc.gpsimd.memset(bias_rows[:], 0.0)
+        nc.vector.memset(w_planes[:].bitcast(I32), 0)
+        nc.scalar.dma_start(out=bias_rows[0:P:BLOCK, :], in_=b.rearrange("(q j) one -> q (j one)", j=BLOCK))
+        nc.vector.transpose(bias[:], bias_rows[:])
 
         planes_of = []
         first_load = True
@@ -47,28 +56,32 @@ def tile_picked_pick_lin_gelu_sub_e_kernel(tc, xT, w_words, w_scales, b, offs, o
                 nc.sync.dma_start(out=raw[:], in_=src[:, r : r + width, :])
                 if first_load:
                     nc.sync.dma_start(offsets[:], offs)
-                    nc.sync.dma_start(out=bias[:], in_=b)
                     first_load = False
                 views.extend(raw[:, i, :] for i in range(width))
                 r += width
             planes_of.append(views)
-        nc.gpsimd.memset(w_planes[:], 0)
         scales_i32 = w_scales.bitcast(I32).rearrange("a q m -> q a m")
         for q in range(4):
             nc.sync.dma_start(out=w_planes[32 * q : 32 * q + 4, :, :].bitcast(I32), in_=scales_i32[4 * q : 4 * q + 4])
         for a in range(PASSES):
             nc.sync.dma_start(out=w_codes[:, a, :].bitcast(I32), in_=w_words[a].rearrange("p m r -> p (m r)").bitcast(I32))
 
-        nc.vector.memset(warm[:], 0.0)
-        nc.scalar.activation(warm_out[:], warm[:], gelu)
-
         grouped = [keep.tile([P, S, PACK], BF16, name=f"grouped_{a}", align_bytes=64) for a in range(PASSES)]
         codes = [keep.tile([P, S], U32, name=f"codes_{a}", align_bytes=64) for a in range(PASSES)]
         planes = [keep.tile([P, S], U8, name=f"planes_{a}", align_bytes=64) for a in range(PASSES)]
-        sums = [psum.tile([N, HALF], F32, name=f"sums_{h}") for h in range(2)]
+        sums = [psum.tile([N, GROUP], F32, name=f"sums_{h}") for h in range(GROUPS)]
 
         def pick(a, r, c0, c1):
             nc.vector.tensor_copy(grouped[a][:, c0:c1, r], planes_of[a][r].indirect(offsets[:, c0 // 16 : c1 // 16]))
+
+        def pick_and_weave(a, count):
+            dense = keep.tile([P, count, S], F32, name=f"dense_{a}")
+            for r in range(count):
+                nc.vector.tensor_copy(dense[:, r, :], planes_of[a][r].indirect(offsets[:]))
+            nc.scalar.copy(
+                grouped[a][:, :, 0:count].rearrange("p (c i) r -> p c r i", i=RUN),
+                dense[:].rearrange("p r (c i) -> p c r i", i=RUN),
+            )
 
         def quantise(a, c0, c1):
             nc.vector.quantize_mx(
@@ -78,7 +91,7 @@ def tile_picked_pick_lin_gelu_sub_e_kernel(tc, xT, w_words, w_scales, b, offs, o
             )
 
         def multiply(a, h):
-            cols = slice(h * HALF, (h + 1) * HALF)
+            cols = slice(h * GROUP, (h + 1) * GROUP)
             nc.tensor.matmul_mx(
                 out=sums[h][:],
                 lhsT=w_codes[:, a, :].bitcast(FP8X4),
@@ -90,20 +103,25 @@ def tile_picked_pick_lin_gelu_sub_e_kernel(tc, xT, w_words, w_scales, b, offs, o
             )
 
         for a in range(PASSES - 1):
-            for r in range(PACK):
+            if WOVEN_ON_SCALAR[a]:
+                pick_and_weave(a, WOVEN_ON_SCALAR[a])
+            for r in range(WOVEN_ON_SCALAR[a], PACK):
                 pick(a, r, 0, S)
             quantise(a, 0, S)
-            for h in range(2):
+            for h in range(GROUPS):
                 multiply(a, h)
 
         a = PASSES - 1
-        for r in range(PACK - 1):
+        pick_and_weave(a, WOVEN_ON_SCALAR[a])
+        for r in range(WOVEN_ON_SCALAR[a], PACK - 1):
             pick(a, r, 0, S)
         for h in range(2):
             pick(a, PACK - 1, h * HALF, (h + 1) * HALF)
-        for h in range(2):
-            quantise(a, h * HALF, (h + 1) * HALF)
-            multiply(a, h)
-            result = keep.tile([N, HALF], F32, name=f"result_{h}")
-            nc.scalar.activation(result[:], sums[h][:], gelu, bias=bias[:])
-            nc.sync.dma_start(out=out[:, h * HALF : (h + 1) * HALF], in_=result[:])
+        results = [keep.tile([N, HALF], F32, name=f"result_{h}") for h in range(2)]
+        for g in range(GROUPS):
+            quantise(a, g * GROUP, (g + 1) * GROUP)
+            multiply(a, g)
+            h, i = divmod(g, 2)
+            nc.scalar.activation(results[h][:, i * GROUP : (i + 1) * GROUP], sums[g][:], gelu, bias=bias[:, 0:1])
+            if i == 1:
+                nc.sync.dma_start(out=out[:, h * HALF : (h + 1) * HALF], in_=results[h][:])

@@ -22,7 +22,6 @@ GROUPS = 4
 GROUP = S // GROUPS
 BLOCK = 32
 LOAD_WIDTHS = ((4,), (2, 2), (2, 1, 1))
-WOVEN_ON_SCALAR = (2, 2, 2)
 RUN = 4
 
 
@@ -51,7 +50,7 @@ def tile_picked_pick_lin_gelu_sub_e_kernel(tc, xT, w_words, w_scales, b, offs, o
             views = []
             r = 0
             for width in LOAD_WIDTHS[a]:
-                raw = keep.tile([P, width, T], F32, name=f"raw_{a}_{r}")
+                raw = keep.tile([P, width, T], F32, name=f"raw_{a}_{r}", align_bytes=64)
                 src = xT[a * K_PASS : (a + 1) * K_PASS, :].rearrange("(p r) t -> p r t", r=PACK)
                 nc.sync.dma_start(out=raw[:], in_=src[:, r : r + width, :])
                 if first_load:
@@ -67,61 +66,57 @@ def tile_picked_pick_lin_gelu_sub_e_kernel(tc, xT, w_words, w_scales, b, offs, o
             nc.sync.dma_start(out=w_codes[:, a, :].bitcast(I32), in_=w_words[a].rearrange("p m r -> p (m r)").bitcast(I32))
 
         grouped = [keep.tile([P, S, PACK], BF16, name=f"grouped_{a}", align_bytes=64) for a in range(PASSES)]
-        codes = [keep.tile([P, S], U32, name=f"codes_{a}", align_bytes=64) for a in range(PASSES)]
         planes = [keep.tile([P, S], U8, name=f"planes_{a}", align_bytes=64) for a in range(PASSES)]
-        sums = [psum.tile([N, GROUP], F32, name=f"sums_{h}") for h in range(GROUPS)]
+        sums = [psum.tile([N, GROUP], F32, name=f"sums_{g}") for g in range(GROUPS)]
+        results = [keep.tile([N, HALF], F32, name=f"result_{h}") for h in range(2)]
 
         def pick(a, r, c0, c1):
             nc.vector.tensor_copy(grouped[a][:, c0:c1, r], planes_of[a][r].indirect(offsets[:, c0 // 16 : c1 // 16]))
 
-        def pick_and_weave(a, count):
-            dense = keep.tile([P, count, S], F32, name=f"dense_{a}")
-            for r in range(count):
-                nc.vector.tensor_copy(dense[:, r, :], planes_of[a][r].indirect(offsets[:]))
+        def pick_pair(a, r):
+            dense = keep.tile([P, 2, S], F32, name=f"dense_{a}_{r}")
+            for i in range(2):
+                nc.vector.tensor_copy(dense[:, i, :], planes_of[a][r + i].indirect(offsets[:]))
             nc.scalar.copy(
-                grouped[a][:, :, 0:count].rearrange("p (c i) r -> p c r i", i=RUN),
+                grouped[a][:, :, r : r + 2].rearrange("p (c i) r -> p c r i", i=RUN),
                 dense[:].rearrange("p r (c i) -> p c r i", i=RUN),
             )
 
-        def quantise(a, c0, c1):
-            nc.vector.quantize_mx(
-                out=codes[a][:, c0:c1].bitcast(FP8X4),
-                scales=planes[a][:, c0:c1],
-                in_=grouped[a][:, c0:c1, :].rearrange("p c r -> p (c r)"),
-            )
+        def pick_stepped(a):
+            pick(a, PACK - 2, 0, S)
+            for h in range(2):
+                pick(a, PACK - 1, h * HALF, (h + 1) * HALF)
 
-        def multiply(a, h):
-            cols = slice(h * GROUP, (h + 1) * GROUP)
-            nc.tensor.matmul_mx(
-                out=sums[h][:],
-                lhsT=w_codes[:, a, :].bitcast(FP8X4),
-                lhsT_scale=w_planes[:, a, :],
-                rhs=codes[a][:, cols].bitcast(FP8X4),
-                rhs_scale=planes[a][:, cols],
-                start=(a == 0),
-                stop=(a == PASSES - 1),
-            )
+        def product(a, codes, width):
+            for c0 in range(0, S, width):
+                nc.vector.quantize_mx(
+                    out=codes[:, c0 : c0 + width].bitcast(FP8X4),
+                    scales=planes[a][:, c0 : c0 + width],
+                    in_=grouped[a][:, c0 : c0 + width, :].rearrange("p c r -> p (c r)"),
+                )
+                for g in range(c0 // GROUP, (c0 + width) // GROUP):
+                    cols = slice(g * GROUP, (g + 1) * GROUP)
+                    nc.tensor.matmul_mx(
+                        out=sums[g][:],
+                        lhsT=w_codes[:, a, :].bitcast(FP8X4),
+                        lhsT_scale=w_planes[:, a, :],
+                        rhs=codes[:, cols].bitcast(FP8X4),
+                        rhs_scale=planes[a][:, cols],
+                        start=(a == 0),
+                        stop=(a == PASSES - 1),
+                    )
+                    if a == PASSES - 1:
+                        h, i = divmod(g, 2)
+                        nc.scalar.activation(results[h][:, i * GROUP : (i + 1) * GROUP], sums[g][:], gelu, bias=bias[:, 0:1])
+                        if i == 1:
+                            nc.sync.dma_start(out=out[:, h * HALF : (h + 1) * HALF], in_=results[h][:])
 
-        for a in range(PASSES - 1):
-            if WOVEN_ON_SCALAR[a]:
-                pick_and_weave(a, WOVEN_ON_SCALAR[a])
-            for r in range(WOVEN_ON_SCALAR[a], PACK):
-                pick(a, r, 0, S)
-            quantise(a, 0, S)
-            for h in range(GROUPS):
-                multiply(a, h)
-
-        a = PASSES - 1
-        pick_and_weave(a, WOVEN_ON_SCALAR[a])
-        for r in range(WOVEN_ON_SCALAR[a], PACK - 1):
-            pick(a, r, 0, S)
-        for h in range(2):
-            pick(a, PACK - 1, h * HALF, (h + 1) * HALF)
-        results = [keep.tile([N, HALF], F32, name=f"result_{h}") for h in range(2)]
-        for g in range(GROUPS):
-            quantise(a, g * GROUP, (g + 1) * GROUP)
-            multiply(a, g)
-            h, i = divmod(g, 2)
-            nc.scalar.activation(results[h][:, i * GROUP : (i + 1) * GROUP], sums[g][:], gelu, bias=bias[:, 0:1])
-            if i == 1:
-                nc.sync.dma_start(out=out[:, h * HALF : (h + 1) * HALF], in_=results[h][:])
+        pick_pair(0, 0)
+        pick_pair(0, 2)
+        pick_pair(1, 0)
+        product(0, keep.tile([P, S], U32, name="codes_0", tag="raw_1_0", align_bytes=64), S)
+        pick_stepped(1)
+        product(1, keep.tile([P, S], U32, name="codes_1", align_bytes=64), HALF)
+        pick_pair(2, 0)
+        pick_stepped(2)
+        product(2, keep.tile([P, S], U32, name="codes_2", align_bytes=64), GROUP)

@@ -17,12 +17,12 @@ P = 128
 PACK = 4
 K_PASS = P * PACK
 PASSES = K // K_PASS
+LAST = PASSES - 1
 HALF = S // 2
 GROUPS = 4
 GROUP = S // GROUPS
 BLOCK = 32
-LOAD_WIDTHS = ((4,), (2, 2), (2, 1, 1))
-RUN = 4
+LOAD_WIDTHS = ((2, 2), (2, 2), (2, 1, 1))
 
 
 def tile_picked_pick_lin_gelu_sub_e_kernel(tc, xT, w_words, w_scales, b, offs, out):
@@ -36,6 +36,7 @@ def tile_picked_pick_lin_gelu_sub_e_kernel(tc, xT, w_words, w_scales, b, offs, o
         offsets = keep.tile([P, S // 16], U16, name="offsets")
         bias_rows = keep.tile([P, BLOCK], F32, name="bias_rows", align_bytes=64)
         bias = keep.tile([P, BLOCK], F32, name="bias", align_bytes=64)
+        warm = keep.tile([P, 1], F32, name="warm")
         w_codes = keep.tile([P, PASSES, N], U32, name="w_codes", align_bytes=64)
         w_planes = keep.tile([P, PASSES, N], U8, name="w_planes", align_bytes=64)
 
@@ -43,8 +44,12 @@ def tile_picked_pick_lin_gelu_sub_e_kernel(tc, xT, w_words, w_scales, b, offs, o
         nc.vector.memset(w_planes[:].bitcast(I32), 0)
         nc.scalar.dma_start(out=bias_rows[0:P:BLOCK, :], in_=b.rearrange("(q j) one -> q (j one)", j=BLOCK))
         nc.vector.transpose(bias[:], bias_rows[:])
+        nc.scalar.activation(warm[:], bias[:, 0:1], gelu)
+        scales_i32 = w_scales.bitcast(I32).rearrange("a q m -> q a m")
+        for q in range(4):
+            nc.gpsimd.dma_start(out=w_planes[32 * q : 32 * q + 4, :, :].bitcast(I32), in_=scales_i32[4 * q : 4 * q + 4])
 
-        planes_of = []
+        slots = []
         first_load = True
         for a in range(PASSES):
             views = []
@@ -58,65 +63,69 @@ def tile_picked_pick_lin_gelu_sub_e_kernel(tc, xT, w_words, w_scales, b, offs, o
                     first_load = False
                 views.extend(raw[:, i, :] for i in range(width))
                 r += width
-            planes_of.append(views)
-        scales_i32 = w_scales.bitcast(I32).rearrange("a q m -> q a m")
-        for q in range(4):
-            nc.sync.dma_start(out=w_planes[32 * q : 32 * q + 4, :, :].bitcast(I32), in_=scales_i32[4 * q : 4 * q + 4])
+            slots.append(views)
         for a in range(PASSES):
             nc.sync.dma_start(out=w_codes[:, a, :].bitcast(I32), in_=w_words[a].rearrange("p m r -> p (m r)").bitcast(I32))
 
-        grouped = [keep.tile([P, S, PACK], BF16, name=f"grouped_{a}", align_bytes=64) for a in range(PASSES)]
+        pairs = [keep.tile([P, 2, S, 2], BF16, name=f"pairs_{a}", align_bytes=64) for a in range(PASSES)]
+        grouped = [[keep.tile([P, HALF, PACK], BF16, name=f"grouped_{a}_{h}", align_bytes=64) for h in range(2)] for a in range(PASSES)]
         planes = [keep.tile([P, S], U8, name=f"planes_{a}", align_bytes=64) for a in range(PASSES)]
         sums = [psum.tile([N, GROUP], F32, name=f"sums_{g}") for g in range(GROUPS)]
         results = [keep.tile([N, HALF], F32, name=f"result_{h}") for h in range(2)]
 
-        def pick(a, r, c0, c1):
-            nc.vector.tensor_copy(grouped[a][:, c0:c1, r], planes_of[a][r].indirect(offsets[:, c0 // 16 : c1 // 16]))
+        def looked_up(a, r, c0, c1):
+            return slots[a][r].indirect(offsets[:, c0 // 16 : c1 // 16])
 
-        def pick_pair(a, r):
-            dense = keep.tile([P, 2, S], F32, name=f"dense_{a}_{r}")
-            for i in range(2):
-                nc.vector.tensor_copy(dense[:, i, :], planes_of[a][r + i].indirect(offsets[:]))
-            nc.scalar.copy(
-                grouped[a][:, :, r : r + 2].rearrange("p (c i) r -> p c r i", i=RUN),
-                dense[:].rearrange("p r (c i) -> p c r i", i=RUN),
-            )
+        def pick_paired(a, r, c0, c1):
+            nc.vector.tensor_copy(pairs[a][:, r // 2, c0:c1, r % 2], looked_up(a, r, c0, c1))
 
-        def pick_stepped(a):
-            pick(a, PACK - 2, 0, S)
-            for h in range(2):
-                pick(a, PACK - 1, h * HALF, (h + 1) * HALF)
+        def pick_grouped(a, r, h):
+            nc.vector.tensor_copy(grouped[a][h][:, :, r], looked_up(a, r, h * HALF, (h + 1) * HALF))
 
-        def product(a, codes, width):
-            for c0 in range(0, S, width):
+        def weave(a, c0, c1, count):
+            h, c = divmod(c0, HALF)
+            words_in = pairs[a][:].rearrange("p u s e -> p (u s e)").bitcast(U32).rearrange("p (u s) -> p s u", u=2)
+            words_out = grouped[a][h][:].rearrange("p s r -> p (s r)").bitcast(U32).rearrange("p (s u) -> p s u", u=2)
+            nc.scalar.copy(words_out[:, c : c + c1 - c0, 0:count], words_in[:, c0:c1, 0:count])
+
+        def product(a, h, codes, width):
+            for c0 in range(0, HALF, width):
                 nc.vector.quantize_mx(
                     out=codes[:, c0 : c0 + width].bitcast(FP8X4),
-                    scales=planes[a][:, c0 : c0 + width],
-                    in_=grouped[a][:, c0 : c0 + width, :].rearrange("p c r -> p (c r)"),
+                    scales=planes[a][:, h * HALF + c0 : h * HALF + c0 + width],
+                    in_=grouped[a][h][:, c0 : c0 + width, :].rearrange("p c r -> p (c r)"),
                 )
-                for g in range(c0 // GROUP, (c0 + width) // GROUP):
-                    cols = slice(g * GROUP, (g + 1) * GROUP)
+                for i in range(c0 // GROUP, (c0 + width) // GROUP):
+                    g = 2 * h + i
                     nc.tensor.matmul_mx(
                         out=sums[g][:],
                         lhsT=w_codes[:, a, :].bitcast(FP8X4),
                         lhsT_scale=w_planes[:, a, :],
-                        rhs=codes[:, cols].bitcast(FP8X4),
-                        rhs_scale=planes[a][:, cols],
+                        rhs=codes[:, i * GROUP : (i + 1) * GROUP].bitcast(FP8X4),
+                        rhs_scale=planes[a][:, g * GROUP : (g + 1) * GROUP],
                         start=(a == 0),
-                        stop=(a == PASSES - 1),
+                        stop=(a == LAST),
                     )
-                    if a == PASSES - 1:
-                        h, i = divmod(g, 2)
+                    if a == LAST:
                         nc.scalar.activation(results[h][:, i * GROUP : (i + 1) * GROUP], sums[g][:], gelu, bias=bias[:, 0:1])
                         if i == 1:
                             nc.sync.dma_start(out=out[:, h * HALF : (h + 1) * HALF], in_=results[h][:])
 
-        pick_pair(0, 0)
-        pick_pair(0, 2)
-        pick_pair(1, 0)
-        product(0, keep.tile([P, S], U32, name="codes_0", tag="raw_1_0", align_bytes=64), S)
-        pick_stepped(1)
-        product(1, keep.tile([P, S], U32, name="codes_1", align_bytes=64), HALF)
-        pick_pair(2, 0)
-        pick_stepped(2)
-        product(2, keep.tile([P, S], U32, name="codes_2", align_bytes=64), GROUP)
+        for a in range(LAST):
+            for r in range(PACK):
+                pick_paired(a, r, 0, S)
+            for h in range(2):
+                weave(a, h * HALF, (h + 1) * HALF, 2)
+            for h in range(2):
+                product(a, h, keep.tile([P, HALF], U32, name=f"codes_{a}_{h}", align_bytes=64), HALF)
+
+        for r in range(2):
+            pick_paired(LAST, r, 0, S)
+        weave(LAST, HALF, S, 1)
+        for r in range(2, PACK):
+            pick_paired(LAST, r, 0, HALF)
+            pick_grouped(LAST, r, 1)
+        for c0 in range(0, HALF, GROUP):
+            weave(LAST, c0, c0 + GROUP, 2)
+        product(LAST, 0, keep.tile([P, HALF], U32, name="codes_last_0", align_bytes=64), GROUP)
+        product(LAST, 1, keep.tile([P, HALF], U32, name="codes_last_1", tag=f"pairs_{LAST}", align_bytes=64), GROUP)

@@ -22,7 +22,7 @@ HALF = S // 2
 GROUPS = 4
 GROUP = S // GROUPS
 BLOCK = 32
-LOAD_WIDTHS = ((2, 2), (2, 2), (2, 1, 1))
+LOAD_WIDTHS = ((4,), (2, 2), (2, 1, 1))
 
 
 def tile_picked_pick_lin_gelu_sub_e_kernel(tc, xT, w_words, w_scales, b, offs, out):
@@ -68,10 +68,9 @@ def tile_picked_pick_lin_gelu_sub_e_kernel(tc, xT, w_words, w_scales, b, offs, o
             nc.sync.dma_start(out=w_codes[:, a, :].bitcast(I32), in_=w_words[a].rearrange("p m r -> p (m r)").bitcast(I32))
 
         pairs = [keep.tile([P, 2, S, 2], BF16, name=f"pairs_{a}", align_bytes=64) for a in range(PASSES)]
-        grouped = [[keep.tile([P, HALF, PACK], BF16, name=f"grouped_{a}_{h}", align_bytes=64) for h in range(2)] for a in range(PASSES)]
+        grouped = [[keep.tile([P, HALF, PACK], BF16, name=f"grouped_{a}_{h}", align_bytes=64) for h in range(2)] for a in range(LAST)]
         planes = [keep.tile([P, S], U8, name=f"planes_{a}", align_bytes=64) for a in range(PASSES)]
         sums = [psum.tile([N, GROUP], F32, name=f"sums_{g}") for g in range(GROUPS)]
-        results = [keep.tile([N, HALF], F32, name=f"result_{h}") for h in range(2)]
 
         def looked_up(a, r, c0, c1):
             return slots[a][r].indirect(offsets[:, c0 // 16 : c1 // 16])
@@ -79,53 +78,70 @@ def tile_picked_pick_lin_gelu_sub_e_kernel(tc, xT, w_words, w_scales, b, offs, o
         def pick_paired(a, r, c0, c1):
             nc.vector.tensor_copy(pairs[a][:, r // 2, c0:c1, r % 2], looked_up(a, r, c0, c1))
 
-        def pick_grouped(a, r, h):
-            nc.vector.tensor_copy(grouped[a][h][:, :, r], looked_up(a, r, h * HALF, (h + 1) * HALF))
-
-        def weave(a, c0, c1, count):
-            h, c = divmod(c0, HALF)
+        def weave(a, dst, c0, c1):
             words_in = pairs[a][:].rearrange("p u s e -> p (u s e)").bitcast(U32).rearrange("p (u s) -> p s u", u=2)
-            words_out = grouped[a][h][:].rearrange("p s r -> p (s r)").bitcast(U32).rearrange("p (s u) -> p s u", u=2)
-            nc.scalar.copy(words_out[:, c : c + c1 - c0, 0:count], words_in[:, c0:c1, 0:count])
+            words_out = dst[:].rearrange("p s r -> p (s r)").bitcast(U32).rearrange("p (s u) -> p s u", u=2)
+            nc.scalar.copy(words_out, words_in[:, c0:c1, :])
 
-        def product(a, h, codes, width):
-            for c0 in range(0, HALF, width):
-                nc.vector.quantize_mx(
-                    out=codes[:, c0 : c0 + width].bitcast(FP8X4),
-                    scales=planes[a][:, h * HALF + c0 : h * HALF + c0 + width],
-                    in_=grouped[a][h][:, c0 : c0 + width, :].rearrange("p c r -> p (c r)"),
-                )
-                for i in range(c0 // GROUP, (c0 + width) // GROUP):
-                    g = 2 * h + i
-                    nc.tensor.matmul_mx(
-                        out=sums[g][:],
-                        lhsT=w_codes[:, a, :].bitcast(FP8X4),
-                        lhsT_scale=w_planes[:, a, :],
-                        rhs=codes[:, i * GROUP : (i + 1) * GROUP].bitcast(FP8X4),
-                        rhs_scale=planes[a][:, g * GROUP : (g + 1) * GROUP],
-                        start=(a == 0),
-                        stop=(a == LAST),
-                    )
-                    if a == LAST:
-                        nc.scalar.activation(results[h][:, i * GROUP : (i + 1) * GROUP], sums[g][:], gelu, bias=bias[:, 0:1])
-                        if i == 1:
-                            nc.sync.dma_start(out=out[:, h * HALF : (h + 1) * HALF], in_=results[h][:])
+        def quantise(a, src, codes, c0, c1):
+            nc.vector.quantize_mx(out=codes.bitcast(FP8X4), scales=planes[a][:, c0:c1], in_=src.rearrange("p c r -> p (c r)"))
 
-        for a in range(LAST):
-            for r in range(PACK):
-                pick_paired(a, r, 0, S)
-            for h in range(2):
-                weave(a, h * HALF, (h + 1) * HALF, 2)
-            for h in range(2):
-                product(a, h, keep.tile([P, HALF], U32, name=f"codes_{a}_{h}", align_bytes=64), HALF)
+        def multiply(a, g, codes):
+            nc.tensor.matmul_mx(
+                out=sums[g][:],
+                lhsT=w_codes[:, a, :].bitcast(FP8X4),
+                lhsT_scale=w_planes[:, a, :],
+                rhs=codes.bitcast(FP8X4),
+                rhs_scale=planes[a][:, g * GROUP : (g + 1) * GROUP],
+                start=(a == 0),
+                stop=(a == LAST),
+            )
 
+        def product(a, h, codes):
+            quantise(a, grouped[a][h][:], codes, h * HALF, (h + 1) * HALF)
+            for i in range(2):
+                multiply(a, 2 * h + i, codes[:, i * GROUP : (i + 1) * GROUP])
+
+        def finish(g, src, codes, result):
+            quantise(LAST, src, codes, g * GROUP, (g + 1) * GROUP)
+            multiply(LAST, g, codes)
+            nc.scalar.activation(result, sums[g][:], gelu, bias=bias[:, 0:1])
+
+        for r in range(PACK):
+            pick_paired(0, r, 0, S)
+        for h in range(2):
+            weave(0, grouped[0][h], h * HALF, (h + 1) * HALF)
         for r in range(2):
-            pick_paired(LAST, r, 0, S)
-        weave(LAST, HALF, S, 1)
+            pick_paired(1, r, 0, S)
+        codes_0 = keep.tile([P, S], U32, name="codes_0", tag="raw_1_0", align_bytes=64)
+        for h in range(2):
+            product(0, h, codes_0[:, h * HALF : (h + 1) * HALF])
+        for r in range(2, PACK):
+            pick_paired(1, r, 0, S)
+        for h in range(2):
+            weave(1, grouped[1][h], h * HALF, (h + 1) * HALF)
+        for h in range(2):
+            product(1, h, keep.tile([P, HALF], U32, name=f"codes_1_{h}", align_bytes=64)[:])
+
+        woven = [keep.tile([P, GROUP, PACK], BF16, name=f"woven_{g}", align_bytes=64) for g in range(2)]
+        stepped = keep.tile([P, HALF, PACK], BF16, name="stepped", align_bytes=64)
+        pair_late = keep.tile([P, HALF, 2], BF16, name="pair_late", align_bytes=64)
+        for r in range(2):
+            nc.vector.tensor_copy(pair_late[:, :, r], looked_up(LAST, r, HALF, S))
+        nc.scalar.copy(stepped[:, :, 0:2], pair_late[:])
+        for r in range(2):
+            pick_paired(LAST, r, 0, HALF)
         for r in range(2, PACK):
             pick_paired(LAST, r, 0, HALF)
-            pick_grouped(LAST, r, 1)
-        for c0 in range(0, HALF, GROUP):
-            weave(LAST, c0, c0 + GROUP, 2)
-        product(LAST, 0, keep.tile([P, HALF], U32, name="codes_last_0", align_bytes=64), GROUP)
-        product(LAST, 1, keep.tile([P, HALF], U32, name="codes_last_1", tag=f"pairs_{LAST}", align_bytes=64), GROUP)
+            nc.vector.tensor_copy(stepped[:, :, r], looked_up(LAST, r, HALF, S))
+        for g in range(2):
+            weave(LAST, woven[g], g * GROUP, (g + 1) * GROUP)
+
+        codes_woven = keep.tile([P, HALF], U32, name="codes_woven", align_bytes=64)
+        codes_stepped = keep.tile([P, HALF], U32, name="codes_stepped", tag=f"pairs_{LAST}", align_bytes=64)
+        for h, codes in enumerate((codes_woven, codes_stepped)):
+            result = keep.tile([N, HALF], F32, name=f"result_{h}")
+            for i in range(2):
+                cols = slice(i * GROUP, (i + 1) * GROUP)
+                finish(2 * h + i, woven[i][:] if h == 0 else stepped[:, cols, :], codes[:, cols], result[:, cols])
+            nc.sync.dma_start(out=out[:, h * HALF : (h + 1) * HALF], in_=result[:])

@@ -21,7 +21,7 @@ LAST = PASSES - 1
 HALF = S // 2
 GROUPS = 4
 GROUP = S // GROUPS
-BLOCK = 32
+STORE_FROM = {1: 0, 3: 2}
 LOAD_WIDTHS = ((4,), (2, 2), (2, 1, 1))
 
 
@@ -34,20 +34,12 @@ def tile_picked_pick_lin_gelu_sub_e_kernel(tc, xT, w_words, w_scales, b, offs, o
         psum = ctx.enter_context(tc.psum_pool(name="psum", bufs=1))
 
         offsets = keep.tile([P, S // 16], U16, name="offsets")
-        bias_rows = keep.tile([P, BLOCK], F32, name="bias_rows", align_bytes=64)
-        bias = keep.tile([P, BLOCK], F32, name="bias", align_bytes=64)
+        bias = keep.tile([P, 1], F32, name="bias")
         warm = keep.tile([P, 1], F32, name="warm")
         w_codes = keep.tile([P, PASSES, N], U32, name="w_codes", align_bytes=64)
         w_planes = keep.tile([P, PASSES, N], U8, name="w_planes", align_bytes=64)
 
-        nc.gpsimd.memset(bias_rows[:], 0.0)
         nc.vector.memset(w_planes[:].bitcast(I32), 0)
-        nc.scalar.dma_start(out=bias_rows[0:P:BLOCK, :], in_=b.rearrange("(q j) one -> q (j one)", j=BLOCK))
-        nc.vector.transpose(bias[:], bias_rows[:])
-        nc.scalar.activation(warm[:], bias[:, 0:1], gelu)
-        scales_i32 = w_scales.bitcast(I32).rearrange("a q m -> q a m")
-        for q in range(4):
-            nc.gpsimd.dma_start(out=w_planes[32 * q : 32 * q + 4, :, :].bitcast(I32), in_=scales_i32[4 * q : 4 * q + 4])
 
         slots = []
         first_load = True
@@ -64,8 +56,14 @@ def tile_picked_pick_lin_gelu_sub_e_kernel(tc, xT, w_words, w_scales, b, offs, o
                 views.extend(raw[:, i, :] for i in range(width))
                 r += width
             slots.append(views)
-        for a in range(PASSES):
-            nc.sync.dma_start(out=w_codes[:, a, :].bitcast(I32), in_=w_words[a].rearrange("p m r -> p (m r)").bitcast(I32))
+        scales_i32 = w_scales.bitcast(I32).rearrange("a q m -> q a m")
+        for q in range(4):
+            nc.sync.dma_start(out=w_planes[32 * q : 32 * q + 4, :, :].bitcast(I32), in_=scales_i32[4 * q : 4 * q + 4])
+        words_i32 = w_words.rearrange("a p m r -> p a (m r)").bitcast(I32)
+        for passes in (slice(0, 1), slice(1, PASSES)):
+            nc.sync.dma_start(out=w_codes[:, passes, :].bitcast(I32), in_=words_i32[:, passes, :])
+        nc.sync.dma_start(out=bias[:], in_=b)
+        nc.scalar.activation(warm[:], slots[0][0][:, 0:1], gelu)
 
         pairs = [keep.tile([P, 2, S, 2], BF16, name=f"pairs_{a}", align_bytes=64) for a in range(PASSES)]
         grouped = [[keep.tile([P, HALF, PACK], BF16, name=f"grouped_{a}_{h}", align_bytes=64) for h in range(2)] for a in range(LAST)]
@@ -139,9 +137,12 @@ def tile_picked_pick_lin_gelu_sub_e_kernel(tc, xT, w_words, w_scales, b, offs, o
 
         codes_woven = keep.tile([P, HALF], U32, name="codes_woven", align_bytes=64)
         codes_stepped = keep.tile([P, HALF], U32, name="codes_stepped", tag=f"pairs_{LAST}", align_bytes=64)
-        for h, codes in enumerate((codes_woven, codes_stepped)):
-            result = keep.tile([N, HALF], F32, name=f"result_{h}")
-            for i in range(2):
-                cols = slice(i * GROUP, (i + 1) * GROUP)
-                finish(2 * h + i, woven[i][:] if h == 0 else stepped[:, cols, :], codes[:, cols], result[:, cols])
-            nc.sync.dma_start(out=out[:, h * HALF : (h + 1) * HALF], in_=result[:])
+        result = keep.tile([N, S], F32, name="result")
+        for g in range(GROUPS):
+            h, i = divmod(g, 2)
+            cols = slice(i * GROUP, (i + 1) * GROUP)
+            src = woven[i][:] if h == 0 else stepped[:, cols, :]
+            finish(g, src, (codes_woven, codes_stepped)[h][:, cols], result[:, g * GROUP : (g + 1) * GROUP])
+            if g in STORE_FROM:
+                stored = slice(STORE_FROM[g] * GROUP, (g + 1) * GROUP)
+                nc.sync.dma_start(out=out[:, stored], in_=result[:, stored])

@@ -40,6 +40,9 @@ def tile_picked_pick_lin_gelu_sub_e_kernel(tc, xT, w_words, w_scales, b, offs, o
         w_planes = keep.tile([P, PASSES, N], U8, name="w_planes", align_bytes=64)
 
         nc.vector.memset(w_planes[:].bitcast(I32), 0)
+        scales_i32 = w_scales.bitcast(I32).rearrange("a q m -> q a m")
+        for q in range(4):
+            nc.scalar.dma_start(out=w_planes[32 * q : 32 * q + 4, :, :].bitcast(I32), in_=scales_i32[4 * q : 4 * q + 4])
 
         slots = []
         first_load = True
@@ -56,9 +59,6 @@ def tile_picked_pick_lin_gelu_sub_e_kernel(tc, xT, w_words, w_scales, b, offs, o
                 views.extend(raw[:, i, :] for i in range(width))
                 r += width
             slots.append(views)
-        scales_i32 = w_scales.bitcast(I32).rearrange("a q m -> q a m")
-        for q in range(4):
-            nc.sync.dma_start(out=w_planes[32 * q : 32 * q + 4, :, :].bitcast(I32), in_=scales_i32[4 * q : 4 * q + 4])
         words_i32 = w_words.rearrange("a p m r -> p a (m r)").bitcast(I32)
         for passes in (slice(0, 1), slice(1, PASSES)):
             nc.sync.dma_start(out=w_codes[:, passes, :].bitcast(I32), in_=words_i32[:, passes, :])

@@ -76,10 +76,10 @@ def tile_picked_pick_lin_gelu_sub_e_kernel(tc, xT, w_words, w_scales, b, offs, o
         def pick_paired(a, r, c0, c1):
             nc.vector.tensor_copy(pairs[a][:, r // 2, c0:c1, r % 2], looked_up(a, r, c0, c1))
 
-        def weave(a, dst, c0, c1):
+        def weave(a, dst, c0, c1, copy=nc.scalar.copy):
             words_in = pairs[a][:].rearrange("p u s e -> p (u s e)").bitcast(U32).rearrange("p (u s) -> p s u", u=2)
             words_out = dst[:].rearrange("p s r -> p (s r)").bitcast(U32).rearrange("p (s u) -> p s u", u=2)
-            nc.scalar.copy(words_out, words_in[:, c0:c1, :])
+            copy(words_out, words_in[:, c0:c1, :])
 
         def quantise(a, src, codes, c0, c1):
             nc.vector.quantize_mx(out=codes.bitcast(FP8X4), scales=planes[a][:, c0:c1], in_=src.rearrange("p c r -> p (c r)"))
@@ -132,8 +132,10 @@ def tile_picked_pick_lin_gelu_sub_e_kernel(tc, xT, w_words, w_scales, b, offs, o
         for r in range(2, PACK):
             pick_paired(LAST, r, 0, HALF)
             nc.vector.tensor_copy(stepped[:, :, r], looked_up(LAST, r, HALF, S))
-        for g in range(2):
-            weave(LAST, woven[g], g * GROUP, (g + 1) * GROUP)
+        shared = GROUP // 2
+        weave(LAST, woven[0], 0, GROUP)
+        weave(LAST, woven[1][:, 0:shared, :], GROUP, GROUP + shared)
+        weave(LAST, woven[1][:, shared:GROUP, :], GROUP + shared, HALF, nc.gpsimd.tensor_copy)
 
         codes_woven = keep.tile([P, HALF], U32, name="codes_woven", align_bytes=64)
         codes_stepped = keep.tile([P, HALF], U32, name="codes_stepped", tag=f"pairs_{LAST}", align_bytes=64)

@@ -21,7 +21,7 @@ LAST = PASSES - 1
 HALF = S // 2
 GROUPS = 4
 GROUP = S // GROUPS
-STORE_FROM = {1: 0, 3: 2}
+STORE_FROM = {0: 0, 3: 1}
 LOAD_WIDTHS = ((4,), (2, 2), (2, 1, 1))
 
 

@@ -18,16 +18,17 @@ PACK = 4
 K_PASS = P * PACK
 PASSES = K // K_PASS
 LAST = PASSES - 1
-HALF = S // 2
 GROUPS = 4
 GROUP = S // GROUPS
+ON_VECTOR = 288
+LOAD_WIDTHS = ((4,), (4,), (2, 1, 1))
 STORE_FROM = {0: 0, 3: 1}
-LOAD_WIDTHS = ((4,), (2, 2), (2, 1, 1))
 
 
 def tile_picked_pick_lin_gelu_sub_e_kernel(tc, xT, w_words, w_scales, b, offs, out):
     nc = tc.nc
     gelu = mybir.ActivationFunctionType.Gelu_apprx_tanh
+    copy = mybir.ActivationFunctionType.Copy
 
     with ExitStack() as ctx:
         keep = ctx.enter_context(tc.tile_pool(name="keep", bufs=1))
@@ -44,107 +45,68 @@ def tile_picked_pick_lin_gelu_sub_e_kernel(tc, xT, w_words, w_scales, b, offs, o
         for q in range(4):
             nc.scalar.dma_start(out=w_planes[32 * q : 32 * q + 4, :, :].bitcast(I32), in_=scales_i32[4 * q : 4 * q + 4])
 
-        slots = []
-        first_load = True
+        loads = []
         for a in range(PASSES):
-            views = []
+            src = xT[a * K_PASS : (a + 1) * K_PASS, :].rearrange("(p r) t -> p r t", r=PACK)
             r = 0
             for width in LOAD_WIDTHS[a]:
                 raw = keep.tile([P, width, T], F32, name=f"raw_{a}_{r}", align_bytes=64)
-                src = xT[a * K_PASS : (a + 1) * K_PASS, :].rearrange("(p r) t -> p r t", r=PACK)
                 nc.sync.dma_start(out=raw[:], in_=src[:, r : r + width, :])
-                if first_load:
+                if not loads:
                     nc.sync.dma_start(offsets[:], offs)
-                    first_load = False
-                views.extend(raw[:, i, :] for i in range(width))
+                loads.append((a, r, width, raw))
                 r += width
-            slots.append(views)
         words_i32 = w_words.rearrange("a p m r -> p a (m r)").bitcast(I32)
         for passes in (slice(0, 1), slice(1, PASSES)):
             nc.sync.dma_start(out=w_codes[:, passes, :].bitcast(I32), in_=words_i32[:, passes, :])
         nc.sync.dma_start(out=bias[:], in_=b)
-        nc.scalar.activation(warm[:], slots[0][0][:, 0:1], gelu)
+        nc.scalar.activation(warm[:], loads[0][3][:, 0, 0:1], gelu)
 
-        pairs = [keep.tile([P, 2, S, 2], BF16, name=f"pairs_{a}", align_bytes=64) for a in range(PASSES)]
-        grouped = [[keep.tile([P, HALF, PACK], BF16, name=f"grouped_{a}_{h}", align_bytes=64) for h in range(2)] for a in range(LAST)]
+        grouped = [keep.tile([P, S, PACK], BF16, name=f"grouped_{a}", align_bytes=64) for a in range(PASSES)]
+        codes = [keep.tile([P, S], U32, name=f"codes_{a}", align_bytes=64) for a in range(PASSES)]
         planes = [keep.tile([P, S], U8, name=f"planes_{a}", align_bytes=64) for a in range(PASSES)]
         sums = [psum.tile([N, GROUP], F32, name=f"sums_{g}") for g in range(GROUPS)]
+        result = keep.tile([N, S], F32, name="result")
 
-        def looked_up(a, r, c0, c1):
-            return slots[a][r].indirect(offsets[:, c0 // 16 : c1 // 16])
+        def quantise(a, c0, c1):
+            nc.vector.quantize_mx(
+                out=codes[a][:, c0:c1].bitcast(FP8X4),
+                scales=planes[a][:, c0:c1],
+                in_=grouped[a][:, c0:c1, :].rearrange("p c r -> p (c r)"),
+            )
 
-        def pick_paired(a, r, c0, c1):
-            nc.vector.tensor_copy(pairs[a][:, r // 2, c0:c1, r % 2], looked_up(a, r, c0, c1))
-
-        def weave(a, dst, c0, c1, copy=nc.scalar.copy):
-            words_in = pairs[a][:].rearrange("p u s e -> p (u s e)").bitcast(U32).rearrange("p (u s) -> p s u", u=2)
-            words_out = dst[:].rearrange("p s r -> p (s r)").bitcast(U32).rearrange("p (s u) -> p s u", u=2)
-            copy(words_out, words_in[:, c0:c1, :])
-
-        def quantise(a, src, codes, c0, c1):
-            nc.vector.quantize_mx(out=codes.bitcast(FP8X4), scales=planes[a][:, c0:c1], in_=src.rearrange("p c r -> p (c r)"))
-
-        def multiply(a, g, codes):
+        def multiply(a, g):
+            cols = slice(g * GROUP, (g + 1) * GROUP)
             nc.tensor.matmul_mx(
                 out=sums[g][:],
                 lhsT=w_codes[:, a, :].bitcast(FP8X4),
                 lhsT_scale=w_planes[:, a, :],
-                rhs=codes.bitcast(FP8X4),
-                rhs_scale=planes[a][:, g * GROUP : (g + 1) * GROUP],
+                rhs=codes[a][:, cols].bitcast(FP8X4),
+                rhs_scale=planes[a][:, cols],
                 start=(a == 0),
                 stop=(a == LAST),
             )
 
-        def product(a, h, codes):
-            quantise(a, grouped[a][h][:], codes, h * HALF, (h + 1) * HALF)
-            for i in range(2):
-                multiply(a, 2 * h + i, codes[:, i * GROUP : (i + 1) * GROUP])
+        for a, r0, width, raw in loads:
+            final = a == LAST and r0 + width == PACK
+            pieces = ((ON_VECTOR, S - GROUP), (S - GROUP, S)) if final else ((ON_VECTOR, S),)
+            for i in range(width):
+                nc.vector.tensor_copy(grouped[a][:, 0:ON_VECTOR, r0 + i], raw[:, i, :].indirect(offsets[:, 0 : ON_VECTOR // 16]))
+            picked = [keep.tile([P, width, c1 - c0], F32, name=f"picked_{a}_{r0}_{c0}") for c0, c1 in pieces]
+            for (c0, c1), dense in zip(pieces, picked):
+                for i in range(width):
+                    nc.scalar.activation(dense[:, i, :], raw[:, i, :].indirect(offsets[:, c0 // 16 : c1 // 16]), copy)
+            for (c0, c1), dense in zip(pieces, picked):
+                nc.scalar.copy(grouped[a][:, c0:c1, r0 : r0 + width], dense[:].rearrange("p r s -> p s r"))
+            if a < LAST:
+                quantise(a, 0, S)
+                for g in range(GROUPS):
+                    multiply(a, g)
 
-        def finish(g, src, codes, result):
-            quantise(LAST, src, codes, g * GROUP, (g + 1) * GROUP)
-            multiply(LAST, g, codes)
-            nc.scalar.activation(result, sums[g][:], gelu, bias=bias[:, 0:1])
-
-        for r in range(PACK):
-            pick_paired(0, r, 0, S)
-        for h in range(2):
-            weave(0, grouped[0][h], h * HALF, (h + 1) * HALF)
-        for r in range(2):
-            pick_paired(1, r, 0, S)
-        codes_0 = keep.tile([P, S], U32, name="codes_0", tag="raw_1_0", align_bytes=64)
-        for h in range(2):
-            product(0, h, codes_0[:, h * HALF : (h + 1) * HALF])
-        for r in range(2, PACK):
-            pick_paired(1, r, 0, S)
-        for h in range(2):
-            weave(1, grouped[1][h], h * HALF, (h + 1) * HALF)
-        for h in range(2):
-            product(1, h, keep.tile([P, HALF], U32, name=f"codes_1_{h}", align_bytes=64)[:])
-
-        woven = [keep.tile([P, GROUP, PACK], BF16, name=f"woven_{g}", align_bytes=64) for g in range(2)]
-        stepped = keep.tile([P, HALF, PACK], BF16, name="stepped", align_bytes=64)
-        pair_late = keep.tile([P, HALF, 2], BF16, name="pair_late", align_bytes=64)
-        for r in range(2):
-            nc.vector.tensor_copy(pair_late[:, :, r], looked_up(LAST, r, HALF, S))
-        nc.scalar.copy(stepped[:, :, 0:2], pair_late[:])
-        for r in range(2):
-            pick_paired(LAST, r, 0, HALF)
-        for r in range(2, PACK):
-            pick_paired(LAST, r, 0, HALF)
-            nc.vector.tensor_copy(stepped[:, :, r], looked_up(LAST, r, HALF, S))
-        shared = GROUP // 2
-        weave(LAST, woven[0], 0, GROUP)
-        weave(LAST, woven[1][:, 0:shared, :], GROUP, GROUP + shared)
-        weave(LAST, woven[1][:, shared:GROUP, :], GROUP + shared, HALF, nc.gpsimd.tensor_copy)
-
-        codes_woven = keep.tile([P, HALF], U32, name="codes_woven", align_bytes=64)
-        codes_stepped = keep.tile([P, HALF], U32, name="codes_stepped", tag=f"pairs_{LAST}", align_bytes=64)
-        result = keep.tile([N, S], F32, name="result")
         for g in range(GROUPS):
-            h, i = divmod(g, 2)
-            cols = slice(i * GROUP, (i + 1) * GROUP)
-            src = woven[i][:] if h == 0 else stepped[:, cols, :]
-            finish(g, src, (codes_woven, codes_stepped)[h][:, cols], result[:, g * GROUP : (g + 1) * GROUP])
+            quantise(LAST, g * GROUP, (g + 1) * GROUP)
+            multiply(LAST, g)
+            nc.scalar.activation(result[:, g * GROUP : (g + 1) * GROUP], sums[g][:], gelu, bias=bias[:, 0:1])
             if g in STORE_FROM:
                 stored = slice(STORE_FROM[g] * GROUP, (g + 1) * GROUP)
                 nc.sync.dma_start(out=out[:, stored], in_=result[:, stored])

@@ -20,7 +20,8 @@ PASSES = K // K_PASS
 LAST = PASSES - 1
 GROUPS = 4
 GROUP = S // GROUPS
-ON_VECTOR = 288
+ON_VECTOR = 256
+ON_GPSIMD = 64
 LOAD_WIDTHS = ((4,), (4,), (2, 1, 1))
 STORE_FROM = {0: 0, 3: 1}
 
@@ -97,7 +98,11 @@ def tile_picked_pick_lin_gelu_sub_e_kernel(tc, xT, w_words, w_scales, b, offs, o
                 for i in range(width):
                     nc.scalar.activation(dense[:, i, :], raw[:, i, :].indirect(offsets[:, c0 // 16 : c1 // 16]), copy)
             for (c0, c1), dense in zip(pieces, picked):
-                nc.scalar.copy(grouped[a][:, c0:c1, r0 : r0 + width], dense[:].rearrange("p r s -> p s r"))
+                helped = ON_GPSIMD if final and c0 == ON_VECTOR else 0
+                woven = dense[:].rearrange("p r s -> p s r")
+                if helped:
+                    nc.gpsimd.tensor_copy(grouped[a][:, c0 : c0 + helped, r0 : r0 + width], woven[:, 0:helped, :])
+                nc.scalar.copy(grouped[a][:, c0 + helped : c1, r0 : r0 + width], woven[:, helped:, :])
             if a < LAST:
                 quantise(a, 0, S)
                 for g in range(GROUPS):

@@ -58,7 +58,7 @@ def tile_picked_pick_lin_gelu_sub_e_kernel(tc, xT, w_words, w_scales, b, offs, o
                 loads.append((a, r, width, raw))
                 r += width
         words_i32 = w_words.rearrange("a p m r -> p a (m r)").bitcast(I32)
-        for passes in (slice(0, 1), slice(1, PASSES)):
+        for passes in (slice(a, a + 1) for a in range(PASSES)):
             nc.sync.dma_start(out=w_codes[:, passes, :].bitcast(I32), in_=words_i32[:, passes, :])
         nc.sync.dma_start(out=bias[:], in_=b)
         nc.scalar.activation(warm[:], loads[0][3][:, 0, 0:1], gelu)
@@ -105,11 +105,13 @@ def tile_picked_pick_lin_gelu_sub_e_kernel(tc, xT, w_words, w_scales, b, offs, o
                 nc.scalar.copy(grouped[a][:, c0 + helped : c1, r0 : r0 + width], woven[:, helped:, :])
             if a < LAST:
                 quantise(a, 0, S)
-                for g in range(GROUPS):
+                for g in range(GROUPS if a == 0 else GROUPS - 1):
                     multiply(a, g)
 
         for g in range(GROUPS):
             quantise(LAST, g * GROUP, (g + 1) * GROUP)
+            if g == 2:
+                multiply(LAST - 1, GROUPS - 1)
             multiply(LAST, g)
             nc.scalar.activation(result[:, g * GROUP : (g + 1) * GROUP], sums[g][:], gelu, bias=bias[:, 0:1])
             if g in STORE_FROM:

@@ -21,7 +21,8 @@ LAST = PASSES - 1
 GROUPS = 4
 GROUP = S // GROUPS
 ON_VECTOR = 256
-ON_GPSIMD = 64
+ON_GPSIMD = 96
+FIRST_PIECE = 160
 LOAD_WIDTHS = ((4,), (4,), (2, 1, 1))
 STORE_FROM = {0: 0, 3: 1}
 
@@ -90,7 +91,7 @@ def tile_picked_pick_lin_gelu_sub_e_kernel(tc, xT, w_words, w_scales, b, offs, o
 
         for a, r0, width, raw in loads:
             final = a == LAST and r0 + width == PACK
-            pieces = ((ON_VECTOR, S - GROUP), (S - GROUP, S)) if final else ((ON_VECTOR, S),)
+            pieces = ((ON_VECTOR, ON_VECTOR + FIRST_PIECE), (ON_VECTOR + FIRST_PIECE, S)) if final else ((ON_VECTOR, S),)
             for i in range(width):
                 nc.vector.tensor_copy(grouped[a][:, 0:ON_VECTOR, r0 + i], raw[:, i, :].indirect(offsets[:, 0 : ON_VECTOR // 16]))
             picked = [keep.tile([P, width, c1 - c0], F32, name=f"picked_{a}_{r0}_{c0}") for c0, c1 in pieces]

@@ -21,8 +21,7 @@ LAST = PASSES - 1
 GROUPS = 4
 GROUP = S // GROUPS
 ON_VECTOR = 256
-ON_GPSIMD = 96
-FIRST_PIECE = 160
+PIECES = ((96, 96), (96, 32), (64, 0))
 LOAD_WIDTHS = ((4,), (4,), (2, 1, 1))
 STORE_FROM = {0: 0, 3: 1}
 
@@ -91,28 +90,28 @@ def tile_picked_pick_lin_gelu_sub_e_kernel(tc, xT, w_words, w_scales, b, offs, o
 
         for a, r0, width, raw in loads:
             final = a == LAST and r0 + width == PACK
-            pieces = ((ON_VECTOR, ON_VECTOR + FIRST_PIECE), (ON_VECTOR + FIRST_PIECE, S)) if final else ((ON_VECTOR, S),)
+            widths = PIECES if final else ((S - ON_VECTOR, 0),)
+            starts = [ON_VECTOR + sum(n for n, h in widths[:i]) for i in range(len(widths))]
+            pieces = [(c0, c0 + n) for c0, (n, h) in zip(starts, widths)]
             for i in range(width):
                 nc.vector.tensor_copy(grouped[a][:, 0:ON_VECTOR, r0 + i], raw[:, i, :].indirect(offsets[:, 0 : ON_VECTOR // 16]))
             picked = [keep.tile([P, width, c1 - c0], F32, name=f"picked_{a}_{r0}_{c0}") for c0, c1 in pieces]
             for (c0, c1), dense in zip(pieces, picked):
                 for i in range(width):
                     nc.scalar.activation(dense[:, i, :], raw[:, i, :].indirect(offsets[:, c0 // 16 : c1 // 16]), copy)
-            for (c0, c1), dense in zip(pieces, picked):
-                helped = ON_GPSIMD if final and c0 == ON_VECTOR else 0
+            for (c0, c1), dense, (n, helped) in zip(pieces, picked, widths):
                 woven = dense[:].rearrange("p r s -> p s r")
                 if helped:
                     nc.gpsimd.tensor_copy(grouped[a][:, c0 : c0 + helped, r0 : r0 + width], woven[:, 0:helped, :])
-                nc.scalar.copy(grouped[a][:, c0 + helped : c1, r0 : r0 + width], woven[:, helped:, :])
+                if helped < n:
+                    nc.scalar.copy(grouped[a][:, c0 + helped : c1, r0 : r0 + width], woven[:, helped:, :])
             if a < LAST:
                 quantise(a, 0, S)
-                for g in range(GROUPS if a == 0 else GROUPS - 1):
+                for g in range(GROUPS):
                     multiply(a, g)
 
         for g in range(GROUPS):
             quantise(LAST, g * GROUP, (g + 1) * GROUP)
-            if g == 2:
-                multiply(LAST - 1, GROUPS - 1)
             multiply(LAST, g)
             nc.scalar.activation(result[:, g * GROUP : (g + 1) * GROUP], sums[g][:], gelu, bias=bias[:, 0:1])
             if g in STORE_FROM:

@@ -23,6 +23,7 @@ GROUP = S // GROUPS
 ON_VECTOR = 256
 PIECES = ((96, 96), (96, 32), (64, 0))
 LOAD_WIDTHS = ((4,), (4,), (2, 1, 1))
+EARLY_SCALES = 1
 STORE_FROM = {0: 0, 3: 1}
 
 
@@ -43,8 +44,12 @@ def tile_picked_pick_lin_gelu_sub_e_kernel(tc, xT, w_words, w_scales, b, offs, o
 
         nc.vector.memset(w_planes[:].bitcast(I32), 0)
         scales_i32 = w_scales.bitcast(I32).rearrange("a q m -> q a m")
-        for q in range(4):
-            nc.scalar.dma_start(out=w_planes[32 * q : 32 * q + 4, :, :].bitcast(I32), in_=scales_i32[4 * q : 4 * q + 4])
+
+        def load_scales(queue, q):
+            queue.dma_start(out=w_planes[32 * q : 32 * q + 4, :, :].bitcast(I32), in_=scales_i32[4 * q : 4 * q + 4])
+
+        for q in range(EARLY_SCALES):
+            load_scales(nc.scalar, q)
 
         loads = []
         for a in range(PASSES):
@@ -60,6 +65,9 @@ def tile_picked_pick_lin_gelu_sub_e_kernel(tc, xT, w_words, w_scales, b, offs, o
         words_i32 = w_words.rearrange("a p m r -> p a (m r)").bitcast(I32)
         for passes in (slice(a, a + 1) for a in range(PASSES)):
             nc.sync.dma_start(out=w_codes[:, passes, :].bitcast(I32), in_=words_i32[:, passes, :])
+            if passes.start == 0:
+                for q in range(EARLY_SCALES, 4):
+                    load_scales(nc.sync, q)
         nc.sync.dma_start(out=bias[:], in_=b)
         nc.scalar.activation(warm[:], loads[0][3][:, 0, 0:1], gelu)
 

@@ -24,7 +24,7 @@ ON_VECTOR = 256
 PIECES = ((96, 96), (96, 32), (64, 0))
 LOAD_WIDTHS = ((4,), (4,), (2, 1, 1))
 EARLY_SCALES = 1
-STORE_FROM = {0: 0, 3: 1}
+STORE_FROM = {0: 0, 1: 1, 3: 2}
 
 
 def tile_picked_pick_lin_gelu_sub_e_kernel(tc, xT, w_words, w_scales, b, offs, out):
@@ -63,7 +63,7 @@ def tile_picked_pick_lin_gelu_sub_e_kernel(tc, xT, w_words, w_scales, b, offs, o
                 loads.append((a, r, width, raw))
                 r += width
         words_i32 = w_words.rearrange("a p m r -> p a (m r)").bitcast(I32)
-        for passes in (slice(a, a + 1) for a in range(PASSES)):
+        for passes in (slice(0, 1), slice(1, PASSES)):
             nc.sync.dma_start(out=w_codes[:, passes, :].bitcast(I32), in_=words_i32[:, passes, :])
             if passes.start == 0:
                 for q in range(EARLY_SCALES, 4):

@@ -39,8 +39,8 @@ def tile_picked_pick_lin_gelu_sub_e_kernel(tc, xT, w_words, w_scales, b, offs, o
         offsets = keep.tile([P, S // 16], U16, name="offsets")
         bias = keep.tile([P, 1], F32, name="bias")
         warm = keep.tile([P, 1], F32, name="warm")
-        w_codes = keep.tile([P, PASSES, N], U32, name="w_codes", align_bytes=64)
-        w_planes = keep.tile([P, PASSES, N], U8, name="w_planes", align_bytes=64)
+        w_codes = keep.tile([P, PASSES, N], U32, name="w_codes", align_bytes=256)
+        w_planes = keep.tile([P, PASSES, N], U8, name="w_planes", align_bytes=256)
 
         nc.vector.memset(w_planes[:].bitcast(I32), 0)
         scales_i32 = w_scales.bitcast(I32).rearrange("a q m -> q a m")
@@ -56,7 +56,7 @@ def tile_picked_pick_lin_gelu_sub_e_kernel(tc, xT, w_words, w_scales, b, offs, o
             src = xT[a * K_PASS : (a + 1) * K_PASS, :].rearrange("(p r) t -> p r t", r=PACK)
             r = 0
             for width in LOAD_WIDTHS[a]:
-                raw = keep.tile([P, width, T], F32, name=f"raw_{a}_{r}", align_bytes=64)
+                raw = keep.tile([P, width, T], F32, name=f"raw_{a}_{r}", align_bytes=256)
                 nc.sync.dma_start(out=raw[:], in_=src[:, r : r + width, :])
                 if not loads:
                     nc.sync.dma_start(offsets[:], offs)
@@ -75,7 +75,7 @@ def tile_picked_pick_lin_gelu_sub_e_kernel(tc, xT, w_words, w_scales, b, offs, o
         codes = [keep.tile([P, S], U32, name=f"codes_{a}", align_bytes=64) for a in range(PASSES)]
         planes = [keep.tile([P, S], U8, name=f"planes_{a}", align_bytes=64) for a in range(PASSES)]
         sums = [psum.tile([N, GROUP], F32, name=f"sums_{g}") for g in range(GROUPS)]
-        result = keep.tile([N, S], F32, name="result")
+        result = keep.tile([N, S], F32, name="result", align_bytes=256)
 
         def quantise(a, c0, c1):
             nc.vector.quantize_mx(

from contextlib import ExitStack

import concourse.mybir as mybir

K, T, S, N = 1536, 2048, 512, 128
FLOPS = 2 * K * S * N

F32 = mybir.dt.float32
BF16 = mybir.dt.bfloat16
I32 = mybir.dt.int32
U32 = mybir.dt.uint32
U16 = mybir.dt.uint16
U8 = mybir.dt.uint8
FP8X4 = mybir.dt.float8_e4m3fn_x4

P = 128
PACK = 4
K_PASS = P * PACK
PASSES = K // K_PASS
LAST = PASSES - 1
GROUPS = 4
GROUP = S // GROUPS
ON_VECTOR = 256
PIECES = ((96, 96), (96, 32), (64, 0))
LOAD_WIDTHS = ((4,), (4,), (2, 1, 1))
EARLY_SCALES = 1
STORE_FROM = {0: 0, 1: 1, 3: 2}


def tile_picked_pick_lin_gelu_sub_e_kernel(tc, xT, w_words, w_scales, b, offs, out):
    nc = tc.nc
    gelu = mybir.ActivationFunctionType.Gelu_apprx_tanh
    copy = mybir.ActivationFunctionType.Copy

    with ExitStack() as ctx:
        keep = ctx.enter_context(tc.tile_pool(name="keep", bufs=1))
        psum = ctx.enter_context(tc.psum_pool(name="psum", bufs=1))

        offsets = keep.tile([P, S // 16], U16, name="offsets")
        bias = keep.tile([P, 1], F32, name="bias")
        warm = keep.tile([P, 1], F32, name="warm")
        w_codes = keep.tile([P, PASSES, N], U32, name="w_codes", align_bytes=256)
        w_planes = keep.tile([P, PASSES, N], U8, name="w_planes", align_bytes=256)

        nc.vector.memset(w_planes[:].bitcast(I32), 0)
        scales_i32 = w_scales.bitcast(I32).rearrange("a q m -> q a m")

        def load_scales(queue, q):
            queue.dma_start(out=w_planes[32 * q : 32 * q + 4, :, :].bitcast(I32), in_=scales_i32[4 * q : 4 * q + 4])

        for q in range(EARLY_SCALES):
            load_scales(nc.scalar, q)

        loads = []
        for a in range(PASSES):
            src = xT[a * K_PASS : (a + 1) * K_PASS, :].rearrange("(p r) t -> p r t", r=PACK)
            r = 0
            for width in LOAD_WIDTHS[a]:
                raw = keep.tile([P, width, T], F32, name=f"raw_{a}_{r}", align_bytes=256)
                nc.sync.dma_start(out=raw[:], in_=src[:, r : r + width, :])
                if not loads:
                    nc.sync.dma_start(offsets[:], offs)
                loads.append((a, r, width, raw))
                r += width
        words_i32 = w_words.rearrange("a p m r -> p a (m r)").bitcast(I32)
        for passes in (slice(0, 1), slice(1, PASSES)):
            nc.sync.dma_start(out=w_codes[:, passes, :].bitcast(I32), in_=words_i32[:, passes, :])
            if passes.start == 0:
                for q in range(EARLY_SCALES, 4):
                    load_scales(nc.sync, q)
        nc.sync.dma_start(out=bias[:], in_=b)
        nc.scalar.activation(warm[:], loads[0][3][:, 0, 0:1], gelu)

        grouped = [keep.tile([P, S, PACK], BF16, name=f"grouped_{a}", align_bytes=64) for a in range(PASSES)]
        codes = [keep.tile([P, S], U32, name=f"codes_{a}", align_bytes=64) for a in range(PASSES)]
        planes = [keep.tile([P, S], U8, name=f"planes_{a}", align_bytes=64) for a in range(PASSES)]
        sums = [psum.tile([N, GROUP], F32, name=f"sums_{g}") for g in range(GROUPS)]
        result = keep.tile([N, S], F32, name="result", align_bytes=256)

        def quantise(a, c0, c1):
            nc.vector.quantize_mx(
                out=codes[a][:, c0:c1].bitcast(FP8X4),
                scales=planes[a][:, c0:c1],
                in_=grouped[a][:, c0:c1, :].rearrange("p c r -> p (c r)"),
            )

        def multiply(a, g):
            cols = slice(g * GROUP, (g + 1) * GROUP)
            nc.tensor.matmul_mx(
                out=sums[g][:],
                lhsT=w_codes[:, a, :].bitcast(FP8X4),
                lhsT_scale=w_planes[:, a, :],
                rhs=codes[a][:, cols].bitcast(FP8X4),
                rhs_scale=planes[a][:, cols],
                start=(a == 0),
                stop=(a == LAST),
            )

        for a, r0, width, raw in loads:
            final = a == LAST and r0 + width == PACK
            widths = PIECES if final else ((S - ON_VECTOR, 0),)
            starts = [ON_VECTOR + sum(n for n, h in widths[:i]) for i in range(len(widths))]
            pieces = [(c0, c0 + n) for c0, (n, h) in zip(starts, widths)]
            for i in range(width):
                nc.vector.tensor_copy(grouped[a][:, 0:ON_VECTOR, r0 + i], raw[:, i, :].indirect(offsets[:, 0 : ON_VECTOR // 16]))
            picked = [keep.tile([P, width, c1 - c0], F32, name=f"picked_{a}_{r0}_{c0}") for c0, c1 in pieces]
            for (c0, c1), dense in zip(pieces, picked):
                for i in range(width):
                    nc.scalar.activation(dense[:, i, :], raw[:, i, :].indirect(offsets[:, c0 // 16 : c1 // 16]), copy)
            for (c0, c1), dense, (n, helped) in zip(pieces, picked, widths):
                woven = dense[:].rearrange("p r s -> p s r")
                if helped:
                    nc.gpsimd.tensor_copy(grouped[a][:, c0 : c0 + helped, r0 : r0 + width], woven[:, 0:helped, :])
                if helped < n:
                    nc.scalar.copy(grouped[a][:, c0 + helped : c1, r0 : r0 + width], woven[:, helped:, :])
            if a < LAST:
                quantise(a, 0, S)
                for g in range(GROUPS):
                    multiply(a, g)

        for g in range(GROUPS):
            quantise(LAST, g * GROUP, (g + 1) * GROUP)
            multiply(LAST, g)
            nc.scalar.activation(result[:, g * GROUP : (g + 1) * GROUP], sums[g][:], gelu, bias=bias[:, 0:1])
            if g in STORE_FROM:
                stored = slice(STORE_FROM[g] * GROUP, (g + 1) * GROUP)
                nc.sync.dma_start(out=out[:, stored], in_=result[:, stored])
